import numpy as np
import ml_dtypes


def mxq(x, axis, fmt="e4m3"):
    dtype, down = {"e4m3": (ml_dtypes.float8_e4m3fn, 7), "e5m2": (ml_dtypes.float8_e5m2, 14)}[fmt]
    v = np.moveaxis(np.asarray(x, np.float32).astype(ml_dtypes.bfloat16).astype(np.float64), axis, -1)
    blocks = v.reshape(v.shape[:-1] + (-1, 32))
    amax = np.abs(blocks).max(-1, keepdims=True)
    byte = np.maximum(np.where(amax > 0, np.frexp(amax)[1] - 1 + 127, 0) - down, 1)
    scale = np.exp2(byte - 127.0)
    codes = (blocks / scale).astype(np.float32).astype(dtype).astype(np.float64)
    return np.moveaxis((codes * scale).reshape(v.shape), -1, axis)


WIDE = False


def mx_kscale(k):
    if not WIDE:
        return np.ones(k)
    levels = np.array([10, -10, 5, -5, 0])
    if k % 512:
        return np.exp2(np.random.permutation(np.resize(levels, k // 32))).repeat(32)
    a = np.empty((k // 512, 16))
    for p in range(k // 512):
        a[p, :8] = np.random.permutation(np.resize(levels, 8))
        for g in range(8):
            far = levels[np.abs(levels - a[p, g]) >= 10]
            a[p, g + 8] = far[np.random.randint(len(far))]
    return np.exp2(a.ravel()).repeat(32)


def f64(x):
    return np.asarray(x).astype(np.float64)


def striped(idx):
    return np.tile(idx.reshape(-1, 16).T, (8, 1)).astype(np.uint16)


def unstriped(offs):
    return offs[:16].T.reshape(-1).astype(np.int64)


E2M1 = np.array([0.0, 0.5, 1.0, 1.5, 2.0, 3.0, 4.0, 6.0, -0.0, -0.5, -1.0, -1.5, -2.0, -3.0, -4.0, -6.0])


def pack_weight(w, fmt):
    k, n = w.shape
    w = f64(np.asarray(w, np.float32).astype(ml_dtypes.bfloat16)).reshape(k // 32, 32, n)
    amax = np.abs(w).max(1)
    if fmt == "e4m3":
        byte = np.frexp(amax)[1] - 1 + 127 - 7
    else:
        mant, ex = np.frexp(amax / 6.0)
        byte = np.where(mant > 0.5, ex, ex - 1) + 127
    byte = np.clip(np.where(amax > 0, byte, 1), 1, 254)
    scaled = (w * np.exp2(127.0 - byte)[:, None, :]).reshape(k, n).astype(np.float32)
    by_word = np.ascontiguousarray(scaled.reshape(k // 512, 128, 4, n).transpose(0, 1, 3, 2))
    if fmt == "e4m3":
        words = by_word.astype(ml_dtypes.float8_e4m3fn).view(np.uint8)
    else:
        c = by_word.astype(ml_dtypes.float4_e2m1fn).view(np.uint8) & 0xF
        words = (c[..., 0::2] | (c[..., 1::2] << 4)).reshape(k // 512, 128, 2 * n)
    return np.ascontiguousarray(words), np.ascontiguousarray(byte.astype(np.uint8).reshape(k // 512, 16, n))


def unpack_weight(words, scales, fmt):
    g, _, n = scales.shape
    words = np.ascontiguousarray(words).reshape(g, 128, n, -1)
    if fmt == "e4m3":
        vals = words.view(ml_dtypes.float8_e4m3fn).astype(np.float64)
    else:
        nib = np.empty((g, 128, n, 4), np.uint8)
        nib[..., 0::2] = words & 0xF
        nib[..., 1::2] = words >> 4
        vals = E2M1[nib]
    vals = vals * np.repeat(np.exp2(scales.astype(np.float64) - 127.0), 8, axis=1)[..., None]
    return vals.transpose(0, 1, 3, 2).reshape(g * 512, n)


K, M, T, S = 512, 256, 4096, 1536


def setup_inputs():
    n = np.random.standard_normal
    s = mx_kscale(K)[:, None]
    v = pack_weight(n((K, T)) * s, "e4m3")
    return {
        "tab_words": v[0],
        "tab_scales": v[1],
        "w": (n((K, M)) / np.sqrt(K) / s).astype(np.float32),
        "gT": n((M, T)).astype(np.float32),
        "offs": striped(np.random.permutation(T)[:S]),
    }


def reference(tab_words, tab_scales, w, gT, offs):
    tab_ = unpack_weight(tab_words, tab_scales, "e4m3")[:, unstriped(offs)]
    w_ = mxq(f64(w), 0, "e4m3")
    y = w_.T @ tab_
    return (y) * f64(gT)[:, unstriped(offs)]

@@ -1,0 +1,95 @@
+from contextlib import ExitStack
+
+import concourse.mybir as mybir
+
+K, M, T, S = 512, 256, 4096, 1536
+FLOPS = 2 * K * M * S
+
+F32 = mybir.dt.float32
+BF16 = mybir.dt.bfloat16
+I32 = mybir.dt.int32
+U32 = mybir.dt.uint32
+U16 = mybir.dt.uint16
+U8 = mybir.dt.uint8
+FP8X4 = mybir.dt.float8_e4m3fn_x4
+MULT = mybir.AluOpType.mult
+
+P = 128
+PACK = 4
+GROUP = 16
+N_TILE = 512
+HALVES = M // P
+GATE_SLICES = ((512, 512, 512), (512, 512, 256, 128, 128))
+STORE_SLICES = ((1536,), (512, 512, 256, 128, 128))
+
+
+def runs(widths):
+    starts = [sum(widths[:i]) for i in range(len(widths))]
+    return [(start, start + width) for start, width in zip(starts, widths)]
+
+
+def tile_list_tabgate_none_kernel(tc, tab_words, tab_scales, w, gT, offs, out):
+    nc = tc.nc
+    with ExitStack() as ctx:
+        keep = ctx.enter_context(tc.tile_pool(name="keep", bufs=1))
+        psum = ctx.enter_context(tc.psum_pool(name="psum", bufs=1))
+
+        offsets = keep.tile([P, S // GROUP], U16, name="offsets")
+        w_raw = keep.tile([P, PACK, M], F32, name="w_raw")
+        w_grouped = keep.tile([P, M, PACK], BF16, name="w_grouped", align_bytes=64)
+        w_codes = keep.tile([P, M], U32, name="w_codes", align_bytes=64)
+        w_scales = keep.tile([P, M], U8, name="w_scales", align_bytes=64)
+        table_words = keep.tile([P, T], I32, name="table_words", align_bytes=64)
+        table_scales = keep.tile([P, T // PACK], I32, name="table_scales", align_bytes=64)
+        gates = [keep.tile([P, T], F32, name="gates%d" % h, align_bytes=64) for h in range(HALVES)]
+        picked_words = keep.tile([P, S], U32, name="picked_words", align_bytes=64)
+        picked_scales = keep.tile([P, S], U8, name="picked_scales", align_bytes=64)
+        sums = [keep.tile([P, S], F32, name="sums%d" % h, align_bytes=64) for h in range(HALVES)]
+        results = [keep.tile([P, S], F32, name="results%d" % h, align_bytes=64) for h in range(HALVES)]
+
+        def list_slice(a, b):
+            return offsets[:, a // GROUP : b // GROUP]
+
+        nc.vector.memset(table_scales[:], 0)
+
+        words_hbm = tab_words[0].rearrange("p t i -> p (t i)").bitcast(I32)
+        scale_rows = tab_scales[0].bitcast(I32).rearrange("(q r) c -> r q c", r=4)
+        nc.sync.dma_start(out=w_raw[:], in_=w.rearrange("(p j) n -> p j n", j=PACK))
+        nc.sync.dma_start(offsets[:], offs)
+        for r in range(4):
+            nc.sync.dma_start(out=table_scales[r:P:32, :], in_=scale_rows[r])
+        nc.sync.dma_start(out=table_words[:], in_=words_hbm)
+        for h in range(HALVES):
+            nc.sync.dma_start(out=gates[h][:], in_=gT[h * P : (h + 1) * P, :])
+
+        nc.vector.tensor_copy(out=w_grouped[:], in_=w_raw[:].rearrange("p j n -> p n j"))
+        nc.vector.quantize_mx(
+            out=w_codes[:].bitcast(FP8X4),
+            scales=w_scales[:],
+            in_=w_grouped[:].rearrange("p n j -> p (n j)"),
+        )
+
+        nc.vector.tensor_copy(picked_scales[:], table_scales[:].bitcast(U8).indirect(offsets[:]))
+        for a in range(0, S, N_TILE):
+            b = a + N_TILE
+            nc.vector.tensor_copy(picked_words[:, a:b], table_words[:].bitcast(U32).indirect(list_slice(a, b)))
+            for h in range(HALVES):
+                acc = psum.tile([P, N_TILE], F32, name="acc%d_%d" % (h, a))
+                nc.tensor.matmul_mx(
+                    out=acc[:],
+                    lhsT=w_codes[:, h * P : (h + 1) * P].bitcast(FP8X4),
+                    lhsT_scale=w_scales[:, h * P : (h + 1) * P],
+                    rhs=picked_words[:, a:b].bitcast(FP8X4),
+                    rhs_scale=picked_scales[:, a:b],
+                    start=True,
+                    stop=True,
+                )
+                nc.scalar.copy(out=sums[h][:, a:b], in_=acc[:])
+
+        for h in range(HALVES):
+            for a, b in runs(GATE_SLICES[h]):
+                nc.vector.tensor_tensor(
+                    results[h][:, a:b], gates[h][:].indirect(list_slice(a, b)), sums[h][:, a:b], MULT
+                )
+                for c, d in [run for run in runs(STORE_SLICES[h]) if a < run[1] <= b]:
+                    nc.sync.dma_start(out=out[h * P : (h + 1) * P, c:d], in_=results[h][:, c:d])

@@ -43,7 +43,8 @@ def tile_list_tabgate_none_kernel(tc, tab_words, tab_scales, w, gT, offs, out):
         table_scales = keep.tile([P, T // PACK], I32, name="table_scales", align_bytes=64)
         gates = [keep.tile([P, T], F32, name="gates%d" % h, align_bytes=64) for h in range(HALVES)]
         picked_words = keep.tile([P, S], U32, name="picked_words", align_bytes=64)
-        picked_scales = keep.tile([P, S], U8, name="picked_scales", align_bytes=64)
+        picked_rows = keep.tile([P, S // PACK], I32, name="picked_rows", align_bytes=64)
+        picked_scales = keep.tile([P, S // PACK], I32, name="picked_scales", align_bytes=64)
         sums = [keep.tile([P, S], F32, name="sums%d" % h, align_bytes=64) for h in range(HALVES)]
         results = [keep.tile([P, S], F32, name="results%d" % h, align_bytes=64) for h in range(HALVES)]
 
@@ -51,36 +52,43 @@ def tile_list_tabgate_none_kernel(tc, tab_words, tab_scales, w, gT, offs, out):
             return offsets[:, a // GROUP : b // GROUP]
 
         nc.vector.memset(table_scales[:], 0)
+        nc.vector.memset(picked_scales[:], 0)
 
         words_hbm = tab_words[0].rearrange("p t i -> p (t i)").bitcast(I32)
-        scale_rows = tab_scales[0].bitcast(I32).rearrange("(q r) c -> r q c", r=4)
         nc.sync.dma_start(out=w_raw[:], in_=w.rearrange("(p j) n -> p j n", j=PACK))
         nc.sync.dma_start(offsets[:], offs)
-        for r in range(4):
-            nc.sync.dma_start(out=table_scales[r:P:32, :], in_=scale_rows[r])
+        nc.sync.dma_start(out=table_scales[32:96:4, :], in_=tab_scales[0].bitcast(I32))
         nc.sync.dma_start(out=table_words[:], in_=words_hbm)
-        for h in range(HALVES):
-            nc.sync.dma_start(out=gates[h][:], in_=gT[h * P : (h + 1) * P, :])
+        nc.sync.dma_start(out=gates[0][:, : T // 2], in_=gT[0:P, : T // 2])
 
-        nc.vector.tensor_copy(out=w_grouped[:], in_=w_raw[:].rearrange("p j n -> p n j"))
+        nc.scalar.copy(out=w_grouped[:], in_=w_raw[:].rearrange("p j n -> p n j"))
+        nc.vector.tensor_copy(picked_rows[:].bitcast(U8), table_scales[:].bitcast(U8).indirect(offsets[:]))
+        for q in range(4):
+            nc.sync.dma_start(
+                out=picked_scales[32 * q : 32 * q + 4, :], in_=picked_rows[32 + 16 * q : 48 + 16 * q : 4, :]
+            )
+        nc.sync.dma_start(out=gates[0][:, T // 2 :], in_=gT[0:P, T // 2 :])
+        nc.sync.dma_start(out=gates[1][:], in_=gT[P : 2 * P, :])
+
         nc.vector.quantize_mx(
             out=w_codes[:].bitcast(FP8X4),
             scales=w_scales[:],
             in_=w_grouped[:].rearrange("p n j -> p (n j)"),
         )
 
-        nc.vector.tensor_copy(picked_scales[:], table_scales[:].bitcast(U8).indirect(offsets[:]))
         for a in range(0, S, N_TILE):
             b = a + N_TILE
             nc.vector.tensor_copy(picked_words[:, a:b], table_words[:].bitcast(U32).indirect(list_slice(a, b)))
-            for h in range(HALVES):
+        for h in range(HALVES):
+            for a in range(0, S, N_TILE):
+                b = a + N_TILE
                 acc = psum.tile([P, N_TILE], F32, name="acc%d_%d" % (h, a))
                 nc.tensor.matmul_mx(
                     out=acc[:],
                     lhsT=w_codes[:, h * P : (h + 1) * P].bitcast(FP8X4),
                     lhsT_scale=w_scales[:, h * P : (h + 1) * P],
                     rhs=picked_words[:, a:b].bitcast(FP8X4),
-                    rhs_scale=picked_scales[:, a:b],
+                    rhs_scale=picked_scales[:].bitcast(U8)[:, a:b],
                     start=True,
                     stop=True,
                 )

@@ -63,10 +63,8 @@ def tile_list_tabgate_none_kernel(tc, tab_words, tab_scales, w, gT, offs, out):
 
         nc.scalar.copy(out=w_grouped[:], in_=w_raw[:].rearrange("p j n -> p n j"))
         nc.vector.tensor_copy(picked_rows[:].bitcast(U8), table_scales[:].bitcast(U8).indirect(offsets[:]))
-        for q in range(4):
-            nc.sync.dma_start(
-                out=picked_scales[32 * q : 32 * q + 4, :], in_=picked_rows[32 + 16 * q : 48 + 16 * q : 4, :]
-            )
+        for r in range(4):
+            nc.sync.dma_start(out=picked_scales[r:P:32, :], in_=picked_rows[32 + 4 * r : 96 : 16, :])
         nc.sync.dma_start(out=gates[0][:, T // 2 :], in_=gT[0:P, T // 2 :])
         nc.sync.dma_start(out=gates[1][:], in_=gT[P : 2 * P, :])
 

@@ -19,8 +19,8 @@ PACK = 4
 GROUP = 16
 N_TILE = 512
 HALVES = M // P
-GATE_SLICES = ((512, 512, 512), (512, 512, 256, 128, 128))
-STORE_SLICES = ((1536,), (512, 512, 256, 128, 128))
+GATE_SLICES = ((512, 512, 512), (768, 384, 256, 128))
+STORE_SLICES = ((1536,), (768, 384, 256, 128))
 
 
 def runs(widths):

@@ -17,9 +17,12 @@ MULT = mybir.AluOpType.mult
 P = 128
 PACK = 4
 GROUP = 16
-N_TILE = 512
 HALVES = M // P
-GATE_SLICES = ((512, 512, 512), (768, 384, 256, 128))
+PARTS = 2
+PART = S // PARTS
+PLANE_ROWS = (0, 8)
+PART_PASSES = (512, 256)
+GATE_SLICES = ((768, 768), (768, 384, 256, 128))
 STORE_SLICES = ((1536,), (768, 384, 256, 128))
 
 
@@ -43,8 +46,8 @@ def tile_list_tabgate_none_kernel(tc, tab_words, tab_scales, w, gT, offs, out):
         table_scales = keep.tile([P, T // PACK], I32, name="table_scales", align_bytes=64)
         gates = [keep.tile([P, T], F32, name="gates%d" % h, align_bytes=64) for h in range(HALVES)]
         picked_words = keep.tile([P, S], U32, name="picked_words", align_bytes=64)
-        picked_rows = keep.tile([P, S // PACK], I32, name="picked_rows", align_bytes=64)
-        picked_scales = keep.tile([P, S // PACK], I32, name="picked_scales", align_bytes=64)
+        picked_rows = [keep.tile([P, PART // PACK], I32, name="picked_rows%d" % u, align_bytes=64) for u in range(PARTS)]
+        picked_scales = [keep.tile([P, PART // PACK], I32, name="picked_scales%d" % u, align_bytes=64) for u in range(PARTS)]
         sums = [keep.tile([P, S], F32, name="sums%d" % h, align_bytes=64) for h in range(HALVES)]
         results = [keep.tile([P, S], F32, name="results%d" % h, align_bytes=64) for h in range(HALVES)]
 
@@ -52,21 +55,26 @@ def tile_list_tabgate_none_kernel(tc, tab_words, tab_scales, w, gT, offs, out):
             return offsets[:, a // GROUP : b // GROUP]
 
         nc.vector.memset(table_scales[:], 0)
-        nc.vector.memset(picked_scales[:], 0)
+        for u in range(PARTS):
+            nc.vector.memset(picked_scales[u][:], 0)
 
         words_hbm = tab_words[0].rearrange("p t i -> p (t i)").bitcast(I32)
         nc.sync.dma_start(out=w_raw[:], in_=w.rearrange("(p j) n -> p j n", j=PACK))
         nc.sync.dma_start(offsets[:], offs)
         nc.sync.dma_start(out=table_scales[32:96:4, :], in_=tab_scales[0].bitcast(I32))
         nc.sync.dma_start(out=table_words[:], in_=words_hbm)
-        nc.sync.dma_start(out=gates[0][:, : T // 2], in_=gT[0:P, : T // 2])
 
         nc.scalar.copy(out=w_grouped[:], in_=w_raw[:].rearrange("p j n -> p n j"))
-        nc.vector.tensor_copy(picked_rows[:].bitcast(U8), table_scales[:].bitcast(U8).indirect(offsets[:]))
-        for r in range(4):
-            nc.sync.dma_start(out=picked_scales[r:P:32, :], in_=picked_rows[32 + 4 * r : 96 : 16, :])
-        nc.sync.dma_start(out=gates[0][:, T // 2 :], in_=gT[0:P, T // 2 :])
-        nc.sync.dma_start(out=gates[1][:], in_=gT[P : 2 * P, :])
+        for u in range(PARTS):
+            nc.vector.tensor_copy(
+                picked_rows[u][:].bitcast(U8),
+                table_scales[:].bitcast(U8).indirect(list_slice(u * PART, (u + 1) * PART)),
+            )
+            for r in range(4):
+                nc.sync.dma_start(
+                    out=picked_scales[u][PLANE_ROWS[u] + r : P : 32, :], in_=picked_rows[u][32 + 4 * r : 96 : 16, :]
+                )
+            nc.sync.dma_start(out=gates[u][:], in_=gT[u * P : (u + 1) * P, :])
 
         nc.vector.quantize_mx(
             out=w_codes[:].bitcast(FP8X4),
@@ -74,23 +82,24 @@ def tile_list_tabgate_none_kernel(tc, tab_words, tab_scales, w, gT, offs, out):
             in_=w_grouped[:].rearrange("p n j -> p (n j)"),
         )
 
-        for a in range(0, S, N_TILE):
-            b = a + N_TILE
+        for u in range(PARTS):
+            a, b = u * PART, (u + 1) * PART
             nc.vector.tensor_copy(picked_words[:, a:b], table_words[:].bitcast(U32).indirect(list_slice(a, b)))
-        for h in range(HALVES):
-            for a in range(0, S, N_TILE):
-                b = a + N_TILE
-                acc = psum.tile([P, N_TILE], F32, name="acc%d_%d" % (h, a))
-                nc.tensor.matmul_mx(
-                    out=acc[:],
-                    lhsT=w_codes[:, h * P : (h + 1) * P].bitcast(FP8X4),
-                    lhsT_scale=w_scales[:, h * P : (h + 1) * P],
-                    rhs=picked_words[:, a:b].bitcast(FP8X4),
-                    rhs_scale=picked_scales[:].bitcast(U8)[:, a:b],
-                    start=True,
-                    stop=True,
-                )
-                nc.scalar.copy(out=sums[h][:, a:b], in_=acc[:])
+        for u in range(PARTS):
+            for h in range(HALVES):
+                for c, d in runs(PART_PASSES):
+                    a, b = u * PART + c, u * PART + d
+                    acc = psum.tile([P, d - c], F32, name="acc%d_%d" % (h, a))
+                    nc.tensor.matmul_mx(
+                        out=acc[:],
+                        lhsT=w_codes[:, h * P : (h + 1) * P].bitcast(FP8X4),
+                        lhsT_scale=w_scales[:, h * P : (h + 1) * P],
+                        rhs=picked_words[:, a:b].bitcast(FP8X4),
+                        rhs_scale=picked_scales[u][:].bitcast(U8)[PLANE_ROWS[u] : P, c:d],
+                        start=True,
+                        stop=True,
+                    )
+                    nc.scalar.copy(out=sums[h][:, a:b], in_=acc[:])
 
         for h in range(HALVES):
             for a, b in runs(GATE_SLICES[h]):

@@ -20,6 +20,8 @@ GROUP = 16
 HALVES = M // P
 PARTS = 2
 PART = S // PARTS
+PAGE = 4096
+BURST = 256
 PLANE_ROWS = (0, 8)
 PART_PASSES = (512, 256)
 GATE_SLICES = ((768, 768), (768, 384, 256, 128))
@@ -38,18 +40,18 @@ def tile_list_tabgate_none_kernel(tc, tab_words, tab_scales, w, gT, offs, out):
         psum = ctx.enter_context(tc.psum_pool(name="psum", bufs=1))
 
         offsets = keep.tile([P, S // GROUP], U16, name="offsets")
-        w_raw = keep.tile([P, PACK, M], F32, name="w_raw")
+        w_raw = keep.tile([P, PACK, M], F32, name="w_raw", align_bytes=PAGE)
         w_grouped = keep.tile([P, M, PACK], BF16, name="w_grouped", align_bytes=64)
         w_codes = keep.tile([P, M], U32, name="w_codes", align_bytes=64)
         w_scales = keep.tile([P, M], U8, name="w_scales", align_bytes=64)
-        table_words = keep.tile([P, T], I32, name="table_words", align_bytes=64)
-        table_scales = keep.tile([P, T // PACK], I32, name="table_scales", align_bytes=64)
-        gates = [keep.tile([P, T], F32, name="gates%d" % h, align_bytes=64) for h in range(HALVES)]
+        table_words = keep.tile([P, T], I32, name="table_words", align_bytes=PAGE)
+        table_scales = keep.tile([P, T // PACK], I32, name="table_scales", align_bytes=PAGE)
+        gates = [keep.tile([P, T], F32, name="gates%d" % h, align_bytes=PAGE) for h in range(HALVES)]
         picked_words = keep.tile([P, S], U32, name="picked_words", align_bytes=64)
-        picked_rows = [keep.tile([P, PART // PACK], I32, name="picked_rows%d" % u, align_bytes=64) for u in range(PARTS)]
-        picked_scales = [keep.tile([P, PART // PACK], I32, name="picked_scales%d" % u, align_bytes=64) for u in range(PARTS)]
+        picked_rows = [keep.tile([P, PART // PACK], I32, name="picked_rows%d" % u, align_bytes=BURST) for u in range(PARTS)]
+        picked_scales = [keep.tile([P, PART // PACK], I32, name="picked_scales%d" % u, align_bytes=BURST) for u in range(PARTS)]
         sums = [keep.tile([P, S], F32, name="sums%d" % h, align_bytes=64) for h in range(HALVES)]
-        results = [keep.tile([P, S], F32, name="results%d" % h, align_bytes=64) for h in range(HALVES)]
+        results = [keep.tile([P, S], F32, name="results%d" % h, align_bytes=PAGE) for h in range(HALVES)]
 
         def list_slice(a, b):
             return offsets[:, a // GROUP : b // GROUP]

@@ -24,8 +24,8 @@ PAGE = 4096
 BURST = 256
 PLANE_ROWS = (0, 8)
 PART_PASSES = (512, 256)
-GATE_SLICES = ((768, 768), (768, 384, 256, 128))
-STORE_SLICES = ((1536,), (768, 384, 256, 128))
+GATE_SLICES = ((768, 768), (640, 384, 256, 128, 128))
+ROW_SETS = 4
 
 
 def runs(widths):
@@ -108,5 +108,8 @@ def tile_list_tabgate_none_kernel(tc, tab_words, tab_scales, w, gT, offs, out):
                 nc.vector.tensor_tensor(
                     results[h][:, a:b], gates[h][:].indirect(list_slice(a, b)), sums[h][:, a:b], MULT
                 )
-                for c, d in [run for run in runs(STORE_SLICES[h]) if a < run[1] <= b]:
-                    nc.sync.dma_start(out=out[h * P : (h + 1) * P, c:d], in_=results[h][:, c:d])
+                if h == HALVES - 1:
+                    nc.sync.dma_start(out=out[h * P : (h + 1) * P, a:b], in_=results[h][:, a:b])
+            if h < HALVES - 1:
+                for r in range(ROW_SETS):
+                    nc.sync.dma_start(out=out[h * P + r : (h + 1) * P : ROW_SETS, :], in_=results[h][r:P:ROW_SETS, :])

@@ -26,6 +26,8 @@ PLANE_ROWS = (0, 8)
 PART_PASSES = (512, 256)
 GATE_SLICES = ((768, 768), (640, 384, 256, 128, 128))
 ROW_SETS = 4
+SUMS_AT = 14 * PAGE
+RESULTS_AT = 30 * PAGE
 
 
 def runs(widths):
@@ -37,6 +39,7 @@ def tile_list_tabgate_none_kernel(tc, tab_words, tab_scales, w, gT, offs, out):
     nc = tc.nc
     with ExitStack() as ctx:
         keep = ctx.enter_context(tc.tile_pool(name="keep", bufs=1))
+        apart = ctx.enter_context(tc.tile_pool(name="apart", bufs=1))
         psum = ctx.enter_context(tc.psum_pool(name="psum", bufs=1))
 
         offsets = keep.tile([P, S // GROUP], U16, name="offsets")
@@ -50,8 +53,11 @@ def tile_list_tabgate_none_kernel(tc, tab_words, tab_scales, w, gT, offs, out):
         picked_words = keep.tile([P, S], U32, name="picked_words", align_bytes=64)
         picked_rows = [keep.tile([P, PART // PACK], I32, name="picked_rows%d" % u, align_bytes=BURST) for u in range(PARTS)]
         picked_scales = [keep.tile([P, PART // PACK], I32, name="picked_scales%d" % u, align_bytes=BURST) for u in range(PARTS)]
-        sums = [keep.tile([P, S], F32, name="sums%d" % h, align_bytes=64) for h in range(HALVES)]
-        results = [keep.tile([P, S], F32, name="results%d" % h, align_bytes=PAGE) for h in range(HALVES)]
+        sums = [apart.tile([P, S], F32, name="sums%d" % h, offset=SUMS_AT + h * 2 * PAGE, align_bytes=PAGE) for h in range(HALVES)]
+        results = [
+            apart.tile([P, S], F32, name="results%d" % h, offset=RESULTS_AT + h * 2 * PAGE, align_bytes=PAGE)
+            for h in range(HALVES)
+        ]
 
         def list_slice(a, b):
             return offsets[:, a // GROUP : b // GROUP]

@@ -24,7 +24,7 @@ PAGE = 4096
 BURST = 256
 PLANE_ROWS = (0, 8)
 PART_PASSES = (512, 256)
-GATE_SLICES = ((768, 768), (640, 384, 256, 128, 128))
+GATE_SLICES = ((768, 512, 256), (640, 384, 256, 128, 128))
 ROW_SETS = 4
 SUMS_AT = 14 * PAGE
 RESULTS_AT = 30 * PAGE

from contextlib import ExitStack

import concourse.mybir as mybir

K, M, T, S = 512, 256, 4096, 1536
FLOPS = 2 * K * M * S

F32 = mybir.dt.float32
BF16 = mybir.dt.bfloat16
I32 = mybir.dt.int32
U32 = mybir.dt.uint32
U16 = mybir.dt.uint16
U8 = mybir.dt.uint8
FP8X4 = mybir.dt.float8_e4m3fn_x4
MULT = mybir.AluOpType.mult

P = 128
PACK = 4
GROUP = 16
HALVES = M // P
PARTS = 2
PART = S // PARTS
PAGE = 4096
BURST = 256
PLANE_ROWS = (0, 8)
PART_PASSES = (512, 256)
GATE_SLICES = ((768, 512, 256), (640, 384, 256, 128, 128))
ROW_SETS = 4
SUMS_AT = 14 * PAGE
RESULTS_AT = 30 * PAGE


def runs(widths):
    starts = [sum(widths[:i]) for i in range(len(widths))]
    return [(start, start + width) for start, width in zip(starts, widths)]


def tile_list_tabgate_none_kernel(tc, tab_words, tab_scales, w, gT, offs, out):
    nc = tc.nc
    with ExitStack() as ctx:
        keep = ctx.enter_context(tc.tile_pool(name="keep", bufs=1))
        apart = ctx.enter_context(tc.tile_pool(name="apart", bufs=1))
        psum = ctx.enter_context(tc.psum_pool(name="psum", bufs=1))

        offsets = keep.tile([P, S // GROUP], U16, name="offsets")
        w_raw = keep.tile([P, PACK, M], F32, name="w_raw", align_bytes=PAGE)
        w_grouped = keep.tile([P, M, PACK], BF16, name="w_grouped", align_bytes=64)
        w_codes = keep.tile([P, M], U32, name="w_codes", align_bytes=64)
        w_scales = keep.tile([P, M], U8, name="w_scales", align_bytes=64)
        table_words = keep.tile([P, T], I32, name="table_words", align_bytes=PAGE)
        table_scales = keep.tile([P, T // PACK], I32, name="table_scales", align_bytes=PAGE)
        gates = [keep.tile([P, T], F32, name="gates%d" % h, align_bytes=PAGE) for h in range(HALVES)]
        picked_words = keep.tile([P, S], U32, name="picked_words", align_bytes=64)
        picked_rows = [keep.tile([P, PART // PACK], I32, name="picked_rows%d" % u, align_bytes=BURST) for u in range(PARTS)]
        picked_scales = [keep.tile([P, PART // PACK], I32, name="picked_scales%d" % u, align_bytes=BURST) for u in range(PARTS)]
        sums = [apart.tile([P, S], F32, name="sums%d" % h, offset=SUMS_AT + h * 2 * PAGE, align_bytes=PAGE) for h in range(HALVES)]
        results = [
            apart.tile([P, S], F32, name="results%d" % h, offset=RESULTS_AT + h * 2 * PAGE, align_bytes=PAGE)
            for h in range(HALVES)
        ]

        def list_slice(a, b):
            return offsets[:, a // GROUP : b // GROUP]

        nc.vector.memset(table_scales[:], 0)
        for u in range(PARTS):
            nc.vector.memset(picked_scales[u][:], 0)

        words_hbm = tab_words[0].rearrange("p t i -> p (t i)").bitcast(I32)
        nc.sync.dma_start(out=w_raw[:], in_=w.rearrange("(p j) n -> p j n", j=PACK))
        nc.sync.dma_start(offsets[:], offs)
        nc.sync.dma_start(out=table_scales[32:96:4, :], in_=tab_scales[0].bitcast(I32))
        nc.sync.dma_start(out=table_words[:], in_=words_hbm)

        nc.scalar.copy(out=w_grouped[:], in_=w_raw[:].rearrange("p j n -> p n j"))
        for u in range(PARTS):
            nc.vector.tensor_copy(
                picked_rows[u][:].bitcast(U8),
                table_scales[:].bitcast(U8).indirect(list_slice(u * PART, (u + 1) * PART)),
            )
            for r in range(4):
                nc.sync.dma_start(
                    out=picked_scales[u][PLANE_ROWS[u] + r : P : 32, :], in_=picked_rows[u][32 + 4 * r : 96 : 16, :]
                )
            nc.sync.dma_start(out=gates[u][:], in_=gT[u * P : (u + 1) * P, :])

        nc.vector.quantize_mx(
            out=w_codes[:].bitcast(FP8X4),
            scales=w_scales[:],
            in_=w_grouped[:].rearrange("p n j -> p (n j)"),
        )

        for u in range(PARTS):
            a, b = u * PART, (u + 1) * PART
            nc.vector.tensor_copy(picked_words[:, a:b], table_words[:].bitcast(U32).indirect(list_slice(a, b)))
        for u in range(PARTS):
            for h in range(HALVES):
                for c, d in runs(PART_PASSES):
                    a, b = u * PART + c, u * PART + d
                    acc = psum.tile([P, d - c], F32, name="acc%d_%d" % (h, a))
                    nc.tensor.matmul_mx(
                        out=acc[:],
                        lhsT=w_codes[:, h * P : (h + 1) * P].bitcast(FP8X4),
                        lhsT_scale=w_scales[:, h * P : (h + 1) * P],
                        rhs=picked_words[:, a:b].bitcast(FP8X4),
                        rhs_scale=picked_scales[u][:].bitcast(U8)[PLANE_ROWS[u] : P, c:d],
                        start=True,
                        stop=True,
                    )
                    nc.scalar.copy(out=sums[h][:, a:b], in_=acc[:])

        for h in range(HALVES):
            for a, b in runs(GATE_SLICES[h]):
                nc.vector.tensor_tensor(
                    results[h][:, a:b], gates[h][:].indirect(list_slice(a, b)), sums[h][:, a:b], MULT
                )
                if h == HALVES - 1:
                    nc.sync.dma_start(out=out[h * P : (h + 1) * P, a:b], in_=results[h][:, a:b])
            if h < HALVES - 1:
                for r in range(ROW_SETS):
                    nc.sync.dma_start(out=out[h * P + r : (h + 1) * P : ROW_SETS, :], in_=results[h][r:P:ROW_SETS, :])
